import numpy as np
import ml_dtypes


def mxq(x, axis, fmt="e4m3"):
    dtype, down = {"e4m3": (ml_dtypes.float8_e4m3fn, 7), "e5m2": (ml_dtypes.float8_e5m2, 14)}[fmt]
    v = np.moveaxis(np.asarray(x, np.float32).astype(ml_dtypes.bfloat16).astype(np.float64), axis, -1)
    blocks = v.reshape(v.shape[:-1] + (-1, 32))
    amax = np.abs(blocks).max(-1, keepdims=True)
    byte = np.maximum(np.where(amax > 0, np.frexp(amax)[1] - 1 + 127, 0) - down, 1)
    scale = np.exp2(byte - 127.0)
    codes = (blocks / scale).astype(np.float32).astype(dtype).astype(np.float64)
    return np.moveaxis((codes * scale).reshape(v.shape), -1, axis)


WIDE = False


def mx_kscale(k):
    if not WIDE:
        return np.ones(k)
    levels = np.array([10, -10, 5, -5, 0])
    if k % 512:
        return np.exp2(np.random.permutation(np.resize(levels, k // 32))).repeat(32)
    a = np.empty((k // 512, 16))
    for p in range(k // 512):
        a[p, :8] = np.random.permutation(np.resize(levels, 8))
        for g in range(8):
            far = levels[np.abs(levels - a[p, g]) >= 10]
            a[p, g + 8] = far[np.random.randint(len(far))]
    return np.exp2(a.ravel()).repeat(32)


def f64(x):
    return np.asarray(x).astype(np.float64)


def striped(idx):
    return np.tile(idx.reshape(-1, 16).T, (8, 1)).astype(np.uint16)


def unstriped(offs):
    return offs[:16].T.reshape(-1).astype(np.int64)


def pack_weight(w):
    k, n = w.shape
    w = f64(np.asarray(w, np.float32).astype(ml_dtypes.bfloat16)).reshape(k // 32, 32, n)
    amax = np.abs(w).max(1)
    byte = np.clip(np.where(amax > 0, np.frexp(amax)[1] - 1 + 127 - 7, 1), 1, 254)
    scaled = (w * np.exp2(127.0 - byte)[:, None, :]).reshape(k, n).astype(np.float32)
    words = np.ascontiguousarray(scaled.reshape(k // 512, 128, 4, n).transpose(0, 1, 3, 2)).astype(ml_dtypes.float8_e4m3fn).view(np.uint8)
    return words, np.ascontiguousarray(byte.astype(np.uint8).reshape(k // 512, 16, n))


def unpack_weight(words, scales):
    g, p, n, _ = words.shape
    vals = np.ascontiguousarray(words).view(ml_dtypes.float8_e4m3fn).astype(np.float64) * np.repeat(np.exp2(scales.astype(np.float64) - 127.0), 8, axis=1)[..., None]
    return vals.transpose(0, 1, 3, 2).reshape(g * 512, n)


def sigmoid(v):
    return 1.0 / (1.0 + np.exp(-np.maximum(v, -700.0)))


K, T, S, D, N, V = 512, 2048, 1024, 8, 128, 128
P = 2 ** 7


def setup_inputs():
    n = np.random.standard_normal
    s = mx_kscale(K)[:, None]
    packed_xT = pack_weight(n((K, T)) * s)
    return {
        "x_words": packed_xT[0],
        "x_scales": packed_xT[1],
        "w1": (n((K, N)) / np.sqrt(K) / s).astype(np.float32),
        "thr": (np.tile(-np.random.uniform(0.2, 1.5, S), (P, 1))).astype(np.float32),
        "mkt": (0.5 * n((N, 1))).astype(np.float32),
        "lgd": (np.tile(np.random.uniform(0.3, 1.0, S), (P, 1))).astype(np.float32),
        "att": (np.tile(np.random.uniform(0.1, 0.4, V) * D, (P, 1))).astype(np.float32),
        "wid": (np.tile(np.random.uniform(0.1, 0.3, V) * D, (P, 1))).astype(np.float32),
        "offs": striped(np.random.permutation(T)[:S]),
    }


def reference(x_words, x_scales, w1, thr, mkt, lgd, att, wid, offs):
    xq = unpack_weight(x_words, x_scales)[:, unstriped(offs)]
    y = mxq(f64(w1), 0, "e4m3").T @ xq
    pd = sigmoid(1.7 * (f64(thr)[:1] - (0.7 * y) + f64(mkt)))
    vl = (pd * (-1.0 * pd + 1.0)) * ((f64(lgd)[:1]) ** 2)
    sdl = np.sqrt(vl.reshape(len(vl), -1, D).sum(axis=2) + 0.02)
    el = pd * f64(lgd)[:1]
    loss = el.reshape(len(el), -1, D).sum(axis=2)
    za = (loss - f64(att)[:1]) / sdl
    zb = (loss - f64(att)[:1] - f64(wid)[:1]) / sdl
    return sdl * (np.log(np.exp(za) + 1.0) - (np.log(np.exp(zb) + 1.0)))

@@ -1,0 +1,183 @@
+from contextlib import ExitStack
+
+import concourse.mybir as mybir
+from concourse.masks import make_identity
+
+K, T, S, D, M, V = 512, 2048, 1024, 8, 128, 128
+FLOPS = 2 * K * M * S
+
+F32 = mybir.dt.float32
+BF16 = mybir.dt.bfloat16
+I32 = mybir.dt.int32
+U32 = mybir.dt.uint32
+U16 = mybir.dt.uint16
+U8 = mybir.dt.uint8
+FP8X4 = mybir.dt.float8_e4m3fn_x4
+ALU = mybir.AluOpType
+ACT = mybir.ActivationFunctionType
+AX = mybir.AxisListType
+
+P = 128
+PACK = 4
+CHUNK = 256
+CHUNKS = S // CHUNK
+TILES = CHUNK // P
+REST = D // TILES
+V_CHUNK = CHUNK // D
+EARLY = CHUNKS - 1
+
+
+def tile_picked_ytranch_soft_p_kernel(tc, x_words, x_scales, w1, thr, mkt, lgd, att, wid, offs, out):
+    nc = tc.nc
+    with ExitStack() as ctx:
+        keep = ctx.enter_context(tc.tile_pool(name="keep", bufs=1))
+        psum = ctx.enter_context(tc.psum_pool(name="psum", bufs=1))
+
+        offsets = keep.tile([P, S // 16], U16, name="offsets")
+        table_scales = keep.tile([P, T], U8, name="table_scales", align_bytes=64)
+        table_words = keep.tile([P, T], U32, name="table_words", align_bytes=64)
+        w_raw = keep.tile([P, PACK, M], F32, name="w_raw")
+        mkt_col = keep.tile([P, 1], F32, name="mkt_col")
+        thr_col = keep.tile([P, CHUNKS, TILES], F32, name="thr_col")
+        lgd_col = keep.tile([P, CHUNKS, TILES], F32, name="lgd_col")
+        ends = keep.tile([P, 2, V], F32, name="ends")
+        wid_sb = keep.tile([P, V], F32, name="wid_sb")
+
+        nc.gpsimd.memset(table_scales[:].bitcast(I32), 0)
+        nc.sync.dma_start(w_raw[:], w1.rearrange("(p j) m -> p j m", j=PACK))
+        nc.sync.dma_start(offsets[:], offs)
+        for quad in range(4):
+            nc.sync.dma_start(
+                table_scales[32 * quad : 32 * quad + 4, :].bitcast(I32),
+                x_scales[0, 4 * quad : 4 * quad + 4, :].bitcast(I32),
+            )
+        nc.sync.dma_start(table_words[:].bitcast(I32), x_words[0].rearrange("p n t -> p (n t)").bitcast(I32))
+        nc.sync.dma_start(mkt_col[:], mkt)
+        nc.sync.dma_start(thr_col[:], thr[0].rearrange("(c p q) -> p c q", c=CHUNKS, q=TILES))
+        nc.sync.dma_start(lgd_col[:], lgd[0].rearrange("(c p q) -> p c q", c=CHUNKS, q=TILES))
+        nc.sync.dma_start(ends[:, 0, :], att)
+        nc.sync.dma_start(wid_sb[:], wid)
+
+        ident = keep.tile([P, P], F32, name="ident")
+        make_identity(nc, ident[:])
+
+        w_bf = keep.tile([P, M, PACK], BF16, name="w_bf", align_bytes=64)
+        w_codes = keep.tile([P, M], U32, name="w_codes", align_bytes=64)
+        w_scales = keep.tile([P, M], U8, name="w_scales", align_bytes=64)
+        nc.scalar.copy(w_bf[:], w_raw[:].rearrange("p j m -> p m j"))
+
+        thr_scaled = keep.tile([P, CHUNKS, TILES], F32, name="thr_scaled")
+        lgd_half = keep.tile([P, CHUNKS, TILES], F32, name="lgd_half")
+        nc.gpsimd.tensor_scalar(thr_scaled[:], thr_col[:], 0.85, 0.0, ALU.mult, ALU.add)
+        nc.gpsimd.tensor_scalar(lgd_half[:], lgd_col[:], 0.5, 0.0, ALU.mult, ALU.add)
+
+        nc.gpsimd.tensor_tensor(ends[:, 1, :], ends[:, 0, :], wid_sb[:], ALU.add)
+
+        picked_scales = [keep.tile([P, 2 * CHUNK], U8, name=f"picked_scales{h}", align_bytes=64) for h in range(2)]
+        picked_words = [keep.tile([P, CHUNK], U32, name=f"picked_words{c}", align_bytes=64) for c in range(CHUNKS)]
+        nc.vector.tensor_copy(picked_scales[0][:], table_scales[:].indirect(offsets[:, 0:32]))
+        nc.vector.quantize_mx(out=w_codes[:].bitcast(FP8X4), scales=w_scales[:], in_=w_bf[:].rearrange("p m j -> p (m j)"))
+        nc.vector.tensor_copy(picked_scales[1][:], table_scales[:].indirect(offsets[:, 32:64]))
+
+        u = [keep.tile([P, TILES, P], F32, name=f"u{c}") for c in range(CHUNKS)]
+        th = [keep.tile([P, TILES, P], F32, name=f"th{c}") for c in range(CHUNKS)]
+        el = [keep.tile([P, TILES, P], F32, name=f"el{c}") for c in range(CHUNKS)]
+        nvl = [keep.tile([P, TILES, P], F32, name=f"nvl{c}") for c in range(CHUNKS)]
+        nvl_early = psum.tile([P, EARLY, P], F32, name="nvl_early")
+        nvl_late = psum.tile([P, P], F32, name="nvl_late")
+
+        def product(c):
+            h, part = divmod(c, 2)
+            nc.vector.tensor_copy(picked_words[c][:], table_words[:].indirect(offsets[:, 16 * c : 16 * c + 16]))
+            y = psum.tile([P, CHUNK], F32, name=f"y{c}", tag=f"bank{c}")
+            nc.tensor.matmul_mx(
+                out=y[:],
+                lhsT=w_codes[:].bitcast(FP8X4),
+                lhsT_scale=w_scales[:],
+                rhs=picked_words[c][:].bitcast(FP8X4),
+                rhs_scale=picked_scales[h][:, CHUNK * part : CHUNK * (part + 1)],
+                start=True,
+                stop=True,
+            )
+            src = y[:].rearrange("m (p q) -> m q p", q=TILES)
+            if c < EARLY:
+                nc.scalar.activation(u[c][:], src, ACT.Identity, bias=mkt_col[:], scale=-0.7)
+            else:
+                nc.vector.tensor_scalar(u[c][:], src, -0.7, mkt_col[:], ALU.mult, ALU.add)
+
+        def probabilities(c):
+            u_t = psum.tile([P, TILES, P], F32, name=f"u_t{c}", tag=f"bank{c}")
+            for q in range(TILES):
+                nc.tensor.transpose(u_t[:, q, :], u[c][:, q, :], ident[:])
+            for q in range(TILES):
+                nc.scalar.activation(th[c][:, q, :], u_t[:, q, :], ACT.Tanh, bias=thr_scaled[:, c, q : q + 1], scale=0.85)
+
+        def moments(c):
+            for q in range(TILES):
+                half = lgd_half[:, c, q : q + 1]
+                nc.vector.tensor_scalar(el[c][:, q, :], th[c][:, q, :], half, half, ALU.mult, ALU.add)
+            for q in range(TILES):
+                nc.vector.scalar_tensor_tensor(
+                    nvl[c][:, q, :], el[c][:, q, :], lgd_col[:, c, q : q + 1], el[c][:, q, :], ALU.subtract, ALU.mult
+                )
+            nvl_sum = nvl_early[:, c, :] if c < EARLY else nvl_late[:]
+            for q in range(TILES):
+                nc.tensor.matmul(nvl_sum, nvl[c][:, q, :], ident[:], start=q == 0, stop=q == TILES - 1, is_transpose=True)
+
+        def losses(c):
+            el_sum = el_early[:, c, :] if c < EARLY else el_late[:]
+            for q in range(TILES):
+                nc.tensor.matmul(el_sum, el[c][:, q, :], ident[:], start=q == 0, stop=q == TILES - 1, is_transpose=True)
+
+        for c in range(CHUNKS):
+            product(c)
+        for c in range(CHUNKS):
+            probabilities(c)
+        for c in range(CHUNKS):
+            moments(c)
+        el_early = psum.tile([P, EARLY, P], F32, name="el_early", tag="bank3")
+        el_late = psum.tile([P, P], F32, name="el_late", tag="bank2")
+        for c in range(CHUNKS):
+            losses(c)
+
+        nvar = keep.tile([P, V], F32, name="nvar")
+        var = keep.tile([P, V], F32, name="var")
+        loss = keep.tile([P, V], F32, name="loss")
+        sdl = keep.tile([P, V], F32, name="sdl")
+        inv_sdl = keep.tile([P, V], F32, name="inv_sdl")
+        over = keep.tile([P, 2, V], F32, name="over")
+        nabs = keep.tile([P, 2, V], F32, name="nabs")
+        nz = keep.tile([P, 2, V], F32, name="nz")
+        ez = keep.tile([P, 2, V], F32, name="ez")
+        lg = keep.tile([P, V], F32, name="lg")
+        relu_b = keep.tile([P, V], F32, name="relu_b")
+        hard = keep.tile([P, V], F32, name="hard")
+        den = keep.tile([P, V], F32, name="den")
+        inv_den = keep.tile([P, V], F32, name="inv_den")
+        ratio = keep.tile([P, V], F32, name="ratio")
+        soft = keep.tile([P, V], F32, name="soft")
+        res = keep.tile([P, V], F32, name="res")
+
+        split = EARLY * V_CHUNK
+        nc.vector.tensor_reduce(nvar[:, :split], nvl_early[:].rearrange("m c (v e) -> m (c v) e", e=REST), AX.X, ALU.add)
+        nc.vector.tensor_reduce(nvar[:, split:], nvl_late[:].rearrange("m (v e) -> m v e", e=REST), AX.X, ALU.add)
+        nc.scalar.activation(inv_sdl[:], nvar[:], ACT.Abs_reciprocal_sqrt, bias=0.02, scale=-1.0)
+        nc.vector.tensor_reduce(loss[:, :split], el_early[:].rearrange("m c (v e) -> m (c v) e", e=REST), AX.X, ALU.add)
+        nc.vector.tensor_reduce(loss[:, split:], el_late[:].rearrange("m (v e) -> m v e", e=REST), AX.X, ALU.add)
+        nc.vector.tensor_scalar(var[:], nvar[:], -1.0, 0.02, ALU.mult, ALU.add)
+        nc.vector.tensor_tensor(over[:], loss[:].unsqueeze(1).to_broadcast([P, 2, V]), ends[:], ALU.subtract)
+        nc.vector.tensor_tensor(sdl[:], var[:], inv_sdl[:], ALU.mult)
+        over_flat = over[:].rearrange("m s v -> m (s v)")
+        nc.vector.scalar_tensor_tensor(nabs[:].rearrange("m s v -> m (s v)"), over_flat, -1.0, over_flat, ALU.mult, ALU.min)
+        nc.vector.tensor_scalar(relu_b[:], over[:, 1, :], 0.0, None, ALU.max)
+        nc.vector.tensor_tensor(nz[:], nabs[:], inv_sdl[:].unsqueeze(1).to_broadcast([P, 2, V]), ALU.mult)
+        nc.vector.scalar_tensor_tensor(hard[:], over[:, 0, :], 0.0, relu_b[:], ALU.max, ALU.subtract)
+        nc.scalar.activation(ez[:, 1, :], nz[:, 1, :], ACT.Exp)
+        nc.scalar.activation(ez[:, 0, :], nz[:, 0, :], ACT.Exp)
+        nc.vector.tensor_scalar(den[:], ez[:, 1, :], 1.0, None, ALU.add)
+        nc.vector.reciprocal(inv_den[:], den[:])
+        nc.vector.scalar_tensor_tensor(ratio[:], ez[:, 0, :], 1.0, inv_den[:], ALU.add, ALU.mult)
+        nc.scalar.activation(lg[:], ratio[:], ACT.Ln)
+        nc.vector.tensor_tensor(soft[:], lg[:], sdl[:], ALU.mult)
+        nc.vector.tensor_tensor(res[:], soft[:], hard[:], ALU.add)
+        nc.sync.dma_start(out, res[:])

@@ -15,16 +15,13 @@ U8 = mybir.dt.uint8
 FP8X4 = mybir.dt.float8_e4m3fn_x4
 ALU = mybir.AluOpType
 ACT = mybir.ActivationFunctionType
-AX = mybir.AxisListType
 
 P = 128
 PACK = 4
 CHUNK = 256
 CHUNKS = S // CHUNK
-TILES = CHUNK // P
-REST = D // TILES
 V_CHUNK = CHUNK // D
-EARLY = CHUNKS - 1
+PAIR = D // CHUNKS
 
 
 def tile_picked_ytranch_soft_p_kernel(tc, x_words, x_scales, w1, thr, mkt, lgd, att, wid, offs, out):
@@ -38,146 +35,129 @@ def tile_picked_ytranch_soft_p_kernel(tc, x_words, x_scales, w1, thr, mkt, lgd, 
         table_words = keep.tile([P, T], U32, name="table_words", align_bytes=64)
         w_raw = keep.tile([P, PACK, M], F32, name="w_raw")
         mkt_col = keep.tile([P, 1], F32, name="mkt_col")
-        thr_col = keep.tile([P, CHUNKS, TILES], F32, name="thr_col")
-        lgd_col = keep.tile([P, CHUNKS, TILES], F32, name="lgd_col")
+        thr_col = keep.tile([P, D], F32, name="thr_col")
+        lgd_col = keep.tile([P, D], F32, name="lgd_col")
         ends = keep.tile([P, 2, V], F32, name="ends")
         wid_sb = keep.tile([P, V], F32, name="wid_sb")
 
         nc.gpsimd.memset(table_scales[:].bitcast(I32), 0)
-        nc.sync.dma_start(w_raw[:], w1.rearrange("(p j) m -> p j m", j=PACK))
         nc.sync.dma_start(offsets[:], offs)
+        nc.sync.dma_start(mkt_col[:], mkt)
         for quad in range(4):
             nc.sync.dma_start(
                 table_scales[32 * quad : 32 * quad + 4, :].bitcast(I32),
                 x_scales[0, 4 * quad : 4 * quad + 4, :].bitcast(I32),
             )
         nc.sync.dma_start(table_words[:].bitcast(I32), x_words[0].rearrange("p n t -> p (n t)").bitcast(I32))
-        nc.sync.dma_start(mkt_col[:], mkt)
-        nc.sync.dma_start(thr_col[:], thr[0].rearrange("(c p q) -> p c q", c=CHUNKS, q=TILES))
-        nc.sync.dma_start(lgd_col[:], lgd[0].rearrange("(c p q) -> p c q", c=CHUNKS, q=TILES))
+        nc.sync.dma_start(w_raw[:], w1.rearrange("(p j) m -> p j m", j=PACK))
+        nc.sync.dma_start(thr_col[:], thr[0].rearrange("(v d) -> v d", d=D))
+        nc.sync.dma_start(lgd_col[:], lgd[0].rearrange("(v d) -> v d", d=D))
         nc.sync.dma_start(ends[:, 0, :], att)
         nc.sync.dma_start(wid_sb[:], wid)
 
         ident = keep.tile([P, P], F32, name="ident")
         make_identity(nc, ident[:])
 
-        w_bf = keep.tile([P, M, PACK], BF16, name="w_bf", align_bytes=64)
+        w_bf = keep.tile([P, M, PACK], BF16, name="w_bf", tag="staged", align_bytes=64)
         w_codes = keep.tile([P, M], U32, name="w_codes", align_bytes=64)
         w_scales = keep.tile([P, M], U8, name="w_scales", align_bytes=64)
         nc.scalar.copy(w_bf[:], w_raw[:].rearrange("p j m -> p m j"))
 
-        thr_scaled = keep.tile([P, CHUNKS, TILES], F32, name="thr_scaled")
-        lgd_half = keep.tile([P, CHUNKS, TILES], F32, name="lgd_half")
-        nc.gpsimd.tensor_scalar(thr_scaled[:], thr_col[:], 0.85, 0.0, ALU.mult, ALU.add)
-        nc.gpsimd.tensor_scalar(lgd_half[:], lgd_col[:], 0.5, 0.0, ALU.mult, ALU.add)
-
-        nc.gpsimd.tensor_tensor(ends[:, 1, :], ends[:, 0, :], wid_sb[:], ALU.add)
+        thr_scaled = keep.tile([P, D], F32, name="thr_scaled")
+        lgd_half = keep.tile([P, D], F32, name="lgd_half")
+        peak = keep.tile([P, D], F32, name="peak")
+        neg_peak = keep.tile([P, D], F32, name="neg_peak")
+        peak_sum = keep.tile([P, 1], F32, name="peak_sum")
+        nc.scalar.mul(thr_scaled[:], thr_col[:], 0.85)
+        nc.scalar.activation(peak[:], lgd_col[:], ACT.Square, scale=0.5, accum_out=peak_sum[:])
+        nc.scalar.mul(lgd_half[:], lgd_col[:], 0.5)
+        nc.scalar.mul(neg_peak[:], peak[:], -1.0)
 
         picked_scales = [keep.tile([P, 2 * CHUNK], U8, name=f"picked_scales{h}", align_bytes=64) for h in range(2)]
-        picked_words = [keep.tile([P, CHUNK], U32, name=f"picked_words{c}", align_bytes=64) for c in range(CHUNKS)]
-        nc.vector.tensor_copy(picked_scales[0][:], table_scales[:].indirect(offsets[:, 0:32]))
+        for h in range(2):
+            nc.vector.tensor_copy(picked_scales[h][:], table_scales[:].indirect(offsets[:, 32 * h : 32 * h + 32]))
         nc.vector.quantize_mx(out=w_codes[:].bitcast(FP8X4), scales=w_scales[:], in_=w_bf[:].rearrange("p m j -> p (m j)"))
-        nc.vector.tensor_copy(picked_scales[1][:], table_scales[:].indirect(offsets[:, 32:64]))
 
-        u = [keep.tile([P, TILES, P], F32, name=f"u{c}") for c in range(CHUNKS)]
-        th = [keep.tile([P, TILES, P], F32, name=f"th{c}") for c in range(CHUNKS)]
-        el = [keep.tile([P, TILES, P], F32, name=f"el{c}") for c in range(CHUNKS)]
-        nvl = [keep.tile([P, TILES, P], F32, name=f"nvl{c}") for c in range(CHUNKS)]
-        nvl_early = psum.tile([P, EARLY, P], F32, name="nvl_early")
-        nvl_late = psum.tile([P, P], F32, name="nvl_late")
+        u = keep.tile([P, D, V], F32, name="u")
+        th = keep.tile([P, D, M], F32, name="th")
+        el = keep.tile([P, D, M], F32, name="el")
+        dip = keep.tile([P, D, M], F32, name="dip")
+        var_sum = psum.tile([P, V], F32, name="var_sum")
+        loss = psum.tile([P, V], F32, name="loss")
 
-        def product(c):
-            h, part = divmod(c, 2)
-            nc.vector.tensor_copy(picked_words[c][:], table_words[:].indirect(offsets[:, 16 * c : 16 * c + 16]))
-            y = psum.tile([P, CHUNK], F32, name=f"y{c}", tag=f"bank{c}")
+        def product(words, first, width, bank, on_vector):
+            h, col = divmod(first, 2 * CHUNK)
+            y = psum.tile([P, width], F32, name=f"y{first}", tag=bank)
             nc.tensor.matmul_mx(
                 out=y[:],
                 lhsT=w_codes[:].bitcast(FP8X4),
                 lhsT_scale=w_scales[:],
-                rhs=picked_words[c][:].bitcast(FP8X4),
-                rhs_scale=picked_scales[h][:, CHUNK * part : CHUNK * (part + 1)],
+                rhs=words.bitcast(FP8X4),
+                rhs_scale=picked_scales[h][:, col : col + width],
                 start=True,
                 stop=True,
             )
-            src = y[:].rearrange("m (p q) -> m q p", q=TILES)
-            if c < EARLY:
-                nc.scalar.activation(u[c][:], src, ACT.Identity, bias=mkt_col[:], scale=-0.7)
+            src = y[:].rearrange("m (v d) -> m d v", d=D)
+            dst = u[:, :, first // D : (first + width) // D]
+            if on_vector:
+                nc.vector.tensor_scalar(dst, src, -0.7, mkt_col[:], ALU.mult, ALU.add)
             else:
-                nc.vector.tensor_scalar(u[c][:], src, -0.7, mkt_col[:], ALU.mult, ALU.add)
-
-        def probabilities(c):
-            u_t = psum.tile([P, TILES, P], F32, name=f"u_t{c}", tag=f"bank{c}")
-            for q in range(TILES):
-                nc.tensor.transpose(u_t[:, q, :], u[c][:, q, :], ident[:])
-            for q in range(TILES):
-                nc.scalar.activation(th[c][:, q, :], u_t[:, q, :], ACT.Tanh, bias=thr_scaled[:, c, q : q + 1], scale=0.85)
-
-        def moments(c):
-            for q in range(TILES):
-                half = lgd_half[:, c, q : q + 1]
-                nc.vector.tensor_scalar(el[c][:, q, :], th[c][:, q, :], half, half, ALU.mult, ALU.add)
-            for q in range(TILES):
-                nc.vector.scalar_tensor_tensor(
-                    nvl[c][:, q, :], el[c][:, q, :], lgd_col[:, c, q : q + 1], el[c][:, q, :], ALU.subtract, ALU.mult
-                )
-            nvl_sum = nvl_early[:, c, :] if c < EARLY else nvl_late[:]
-            for q in range(TILES):
-                nc.tensor.matmul(nvl_sum, nvl[c][:, q, :], ident[:], start=q == 0, stop=q == TILES - 1, is_transpose=True)
-
-        def losses(c):
-            el_sum = el_early[:, c, :] if c < EARLY else el_late[:]
-            for q in range(TILES):
-                nc.tensor.matmul(el_sum, el[c][:, q, :], ident[:], start=q == 0, stop=q == TILES - 1, is_transpose=True)
+                nc.scalar.activation(dst, src, ACT.Identity, bias=mkt_col[:], scale=-0.7)
 
         for c in range(CHUNKS):
-            product(c)
-        for c in range(CHUNKS):
-            probabilities(c)
-        for c in range(CHUNKS):
-            moments(c)
-        el_early = psum.tile([P, EARLY, P], F32, name="el_early", tag="bank3")
-        el_late = psum.tile([P, P], F32, name="el_late", tag="bank2")
-        for c in range(CHUNKS):
-            losses(c)
+            last = c == CHUNKS - 1
+            words = keep.tile([P, CHUNK], U32, name=f"picked_words{c}", tag="staged" if last else f"words{c}", align_bytes=64)
+            nc.vector.tensor_copy(words[:], table_words[:].indirect(offsets[:, 16 * c : 16 * c + 16]))
+            if last:
+                product(words[:, :P], CHUNK * c, P, "bank3", True)
+                product(words[:, P:], CHUNK * c + P, P, "bank4", False)
+            else:
+                product(words[:], CHUNK * c, CHUNK, f"bank{c}", c == CHUNKS - 2)
+        nc.vector.tensor_tensor(ends[:, 1, :], ends[:, 0, :], wid_sb[:], ALU.add)
 
-        nvar = keep.tile([P, V], F32, name="nvar")
-        var = keep.tile([P, V], F32, name="var")
-        loss = keep.tile([P, V], F32, name="loss")
+        for bank, members in (("bank5", (0,)), ("bank0", (1,)), ("bank1", (2, 3)), ("bank2", (4, 5)), ("bank3", (6, 7))):
+            u_t = psum.tile([P, len(members), M], F32, name=f"u_t{members[0]}", tag=bank)
+            for e, d in enumerate(members):
+                nc.tensor.transpose(u_t[:, e, :], u[:, d, :], ident[:])
+            for e, d in enumerate(members):
+                nc.scalar.activation(th[:, d, :], u_t[:, e, :], ACT.Tanh, bias=thr_scaled[:, d : d + 1], scale=0.85)
+
+        nc.tensor.matmul(var_sum[:], peak_sum[:].to_broadcast([P, M]), ident[:], start=True, stop=False, is_transpose=True)
+        for d in range(D):
+            nc.vector.scalar_tensor_tensor(dip[:, d, :], th[:, d, :], neg_peak[:, d : d + 1], th[:, d, :], ALU.mult, ALU.mult)
+            nc.tensor.matmul(var_sum[:], dip[:, d, :], ident[:], start=False, stop=d == D - 1, is_transpose=True)
+        for d in range(D):
+            half = lgd_half[:, d : d + 1]
+            nc.vector.tensor_scalar(el[:, d, :], th[:, d, :], half, half, ALU.mult, ALU.add)
+            nc.tensor.matmul(loss[:], el[:, d, :], ident[:], start=d == 0, stop=d == D - 1, is_transpose=True)
+
         sdl = keep.tile([P, V], F32, name="sdl")
         inv_sdl = keep.tile([P, V], F32, name="inv_sdl")
         over = keep.tile([P, 2, V], F32, name="over")
-        nabs = keep.tile([P, 2, V], F32, name="nabs")
-        nz = keep.tile([P, 2, V], F32, name="nz")
-        ez = keep.tile([P, 2, V], F32, name="ez")
+        dist = keep.tile([P, 2, V], F32, name="dist")
+        z_abs = keep.tile([P, 2, V], F32, name="z_abs")
+        sig = keep.tile([P, 2, V], F32, name="sig")
         lg = keep.tile([P, V], F32, name="lg")
         relu_b = keep.tile([P, V], F32, name="relu_b")
         hard = keep.tile([P, V], F32, name="hard")
-        den = keep.tile([P, V], F32, name="den")
-        inv_den = keep.tile([P, V], F32, name="inv_den")
+        inv_sig = keep.tile([P, V], F32, name="inv_sig")
         ratio = keep.tile([P, V], F32, name="ratio")
         soft = keep.tile([P, V], F32, name="soft")
         res = keep.tile([P, V], F32, name="res")
 
-        split = EARLY * V_CHUNK
-        nc.vector.tensor_reduce(nvar[:, :split], nvl_early[:].rearrange("m c (v e) -> m (c v) e", e=REST), AX.X, ALU.add)
-        nc.vector.tensor_reduce(nvar[:, split:], nvl_late[:].rearrange("m (v e) -> m v e", e=REST), AX.X, ALU.add)
-        nc.scalar.activation(inv_sdl[:], nvar[:], ACT.Abs_reciprocal_sqrt, bias=0.02, scale=-1.0)
-        nc.vector.tensor_reduce(loss[:, :split], el_early[:].rearrange("m c (v e) -> m (c v) e", e=REST), AX.X, ALU.add)
-        nc.vector.tensor_reduce(loss[:, split:], el_late[:].rearrange("m (v e) -> m v e", e=REST), AX.X, ALU.add)
-        nc.vector.tensor_scalar(var[:], nvar[:], -1.0, 0.02, ALU.mult, ALU.add)
+        nc.scalar.activation(inv_sdl[:], var_sum[:], ACT.Abs_reciprocal_sqrt, bias=0.02)
         nc.vector.tensor_tensor(over[:], loss[:].unsqueeze(1).to_broadcast([P, 2, V]), ends[:], ALU.subtract)
-        nc.vector.tensor_tensor(sdl[:], var[:], inv_sdl[:], ALU.mult)
         over_flat = over[:].rearrange("m s v -> m (s v)")
-        nc.vector.scalar_tensor_tensor(nabs[:].rearrange("m s v -> m (s v)"), over_flat, -1.0, over_flat, ALU.mult, ALU.min)
-        nc.vector.tensor_scalar(relu_b[:], over[:, 1, :], 0.0, None, ALU.max)
-        nc.vector.tensor_tensor(nz[:], nabs[:], inv_sdl[:].unsqueeze(1).to_broadcast([P, 2, V]), ALU.mult)
-        nc.vector.scalar_tensor_tensor(hard[:], over[:, 0, :], 0.0, relu_b[:], ALU.max, ALU.subtract)
-        nc.scalar.activation(ez[:, 1, :], nz[:, 1, :], ACT.Exp)
-        nc.scalar.activation(ez[:, 0, :], nz[:, 0, :], ACT.Exp)
-        nc.vector.tensor_scalar(den[:], ez[:, 1, :], 1.0, None, ALU.add)
-        nc.vector.reciprocal(inv_den[:], den[:])
-        nc.vector.scalar_tensor_tensor(ratio[:], ez[:, 0, :], 1.0, inv_den[:], ALU.add, ALU.mult)
+        nc.vector.scalar_tensor_tensor(dist[:].rearrange("m s v -> m (s v)"), over_flat, -1.0, over_flat, ALU.mult, ALU.max)
+        nc.vector.tensor_tensor(z_abs[:], dist[:], inv_sdl[:].unsqueeze(1).to_broadcast([P, 2, V]), ALU.mult)
+        nc.scalar.activation(sig[:, 0, :], z_abs[:, 0, :], ACT.Sigmoid)
+        nc.scalar.activation(sig[:, 1, :], z_abs[:, 1, :], ACT.Sigmoid)
+        nc.vector.reciprocal(inv_sig[:], sig[:, 0, :])
+        nc.vector.tensor_tensor(ratio[:], sig[:, 1, :], inv_sig[:], ALU.mult)
         nc.scalar.activation(lg[:], ratio[:], ACT.Ln)
+        nc.vector.scalar_tensor_tensor(sdl[:], var_sum[:], 0.02, inv_sdl[:], ALU.add, ALU.mult)
+        nc.vector.tensor_scalar(relu_b[:], over[:, 1, :], 0.0, None, ALU.max)
+        nc.vector.scalar_tensor_tensor(hard[:], over[:, 0, :], 0.0, relu_b[:], ALU.max, ALU.subtract)
         nc.vector.tensor_tensor(soft[:], lg[:], sdl[:], ALU.mult)
         nc.vector.tensor_tensor(res[:], soft[:], hard[:], ALU.add)
         nc.sync.dma_start(out, res[:])

@@ -15,13 +15,16 @@ U8 = mybir.dt.uint8
 FP8X4 = mybir.dt.float8_e4m3fn_x4
 ALU = mybir.AluOpType
 ACT = mybir.ActivationFunctionType
+AX = mybir.AxisListType
 
 P = 128
 PACK = 4
 CHUNK = 256
 CHUNKS = S // CHUNK
-V_CHUNK = CHUNK // D
-PAIR = D // CHUNKS
+HALVES = 2
+HALF = S // HALVES
+TILES = HALF // P
+REST = D // TILES
 
 
 def tile_picked_ytranch_soft_p_kernel(tc, x_words, x_scales, w1, thr, mkt, lgd, att, wid, offs, out):
@@ -35,24 +38,21 @@ def tile_picked_ytranch_soft_p_kernel(tc, x_words, x_scales, w1, thr, mkt, lgd, 
         table_words = keep.tile([P, T], U32, name="table_words", align_bytes=64)
         w_raw = keep.tile([P, PACK, M], F32, name="w_raw")
         mkt_col = keep.tile([P, 1], F32, name="mkt_col")
-        thr_col = keep.tile([P, D], F32, name="thr_col")
-        lgd_col = keep.tile([P, D], F32, name="lgd_col")
+        thr_col = keep.tile([P, HALVES, TILES], F32, name="thr_col")
+        lgd_col = keep.tile([P, HALVES, TILES], F32, name="lgd_col")
         ends = keep.tile([P, 2, V], F32, name="ends")
         wid_sb = keep.tile([P, V], F32, name="wid_sb")
 
         nc.gpsimd.memset(table_scales[:].bitcast(I32), 0)
         nc.sync.dma_start(offsets[:], offs)
-        nc.sync.dma_start(mkt_col[:], mkt)
-        for quad in range(4):
-            nc.sync.dma_start(
-                table_scales[32 * quad : 32 * quad + 4, :].bitcast(I32),
-                x_scales[0, 4 * quad : 4 * quad + 4, :].bitcast(I32),
-            )
+        nc.sync.dma_start(ends[:, 0, :], att)
+        for r in range(4):
+            nc.sync.dma_start(table_scales[r:P:32, :].bitcast(I32), x_scales[0, r:16:4, :].bitcast(I32))
         nc.sync.dma_start(table_words[:].bitcast(I32), x_words[0].rearrange("p n t -> p (n t)").bitcast(I32))
         nc.sync.dma_start(w_raw[:], w1.rearrange("(p j) m -> p j m", j=PACK))
-        nc.sync.dma_start(thr_col[:], thr[0].rearrange("(v d) -> v d", d=D))
-        nc.sync.dma_start(lgd_col[:], lgd[0].rearrange("(v d) -> v d", d=D))
-        nc.sync.dma_start(ends[:, 0, :], att)
+        nc.sync.dma_start(mkt_col[:], mkt)
+        nc.sync.dma_start(thr_col[:], thr[0].rearrange("(h p q) -> p h q", h=HALVES, q=TILES))
+        nc.sync.dma_start(lgd_col[:], lgd[0].rearrange("(h p q) -> p h q", h=HALVES, q=TILES))
         nc.sync.dma_start(wid_sb[:], wid)
 
         ident = keep.tile([P, P], F32, name="ident")
@@ -63,13 +63,14 @@ def tile_picked_ytranch_soft_p_kernel(tc, x_words, x_scales, w1, thr, mkt, lgd, 
         w_scales = keep.tile([P, M], U8, name="w_scales", align_bytes=64)
         nc.scalar.copy(w_bf[:], w_raw[:].rearrange("p j m -> p m j"))
 
-        thr_scaled = keep.tile([P, D], F32, name="thr_scaled")
-        lgd_half = keep.tile([P, D], F32, name="lgd_half")
-        peak = keep.tile([P, D], F32, name="peak")
-        neg_peak = keep.tile([P, D], F32, name="neg_peak")
-        peak_sum = keep.tile([P, 1], F32, name="peak_sum")
+        thr_scaled = keep.tile([P, HALVES, TILES], F32, name="thr_scaled")
+        lgd_half = keep.tile([P, HALVES, TILES], F32, name="lgd_half")
+        peak = keep.tile([P, HALVES, TILES], F32, name="peak")
+        neg_peak = keep.tile([P, HALVES, TILES], F32, name="neg_peak")
+        peak_sum = keep.tile([P, HALVES], F32, name="peak_sum")
         nc.scalar.mul(thr_scaled[:], thr_col[:], 0.85)
-        nc.scalar.activation(peak[:], lgd_col[:], ACT.Square, scale=0.5, accum_out=peak_sum[:])
+        for h in range(HALVES):
+            nc.scalar.activation(peak[:, h, :], lgd_col[:, h, :], ACT.Square, scale=0.5, accum_out=peak_sum[:, h : h + 1])
         nc.scalar.mul(lgd_half[:], lgd_col[:], 0.5)
         nc.scalar.mul(neg_peak[:], peak[:], -1.0)
 
@@ -78,12 +79,12 @@ def tile_picked_ytranch_soft_p_kernel(tc, x_words, x_scales, w1, thr, mkt, lgd, 
             nc.vector.tensor_copy(picked_scales[h][:], table_scales[:].indirect(offsets[:, 32 * h : 32 * h + 32]))
         nc.vector.quantize_mx(out=w_codes[:].bitcast(FP8X4), scales=w_scales[:], in_=w_bf[:].rearrange("p m j -> p (m j)"))
 
-        u = keep.tile([P, D, V], F32, name="u")
-        th = keep.tile([P, D, M], F32, name="th")
-        el = keep.tile([P, D, M], F32, name="el")
-        dip = keep.tile([P, D, M], F32, name="dip")
-        var_sum = psum.tile([P, V], F32, name="var_sum")
-        loss = psum.tile([P, V], F32, name="loss")
+        u = keep.tile([P, HALVES, TILES, P], F32, name="u")
+        th = keep.tile([P, HALVES, TILES, M], F32, name="th")
+        el = keep.tile([P, HALVES, TILES, M], F32, name="el")
+        dip = keep.tile([P, HALVES, TILES, M], F32, name="dip")
+        var_sum = psum.tile([P, HALVES, P], F32, name="var_sum")
+        el_sum = psum.tile([P, HALVES, P], F32, name="el_sum")
 
         def product(words, first, width, bank, on_vector):
             h, col = divmod(first, 2 * CHUNK)
@@ -97,8 +98,8 @@ def tile_picked_ytranch_soft_p_kernel(tc, x_words, x_scales, w1, thr, mkt, lgd, 
                 start=True,
                 stop=True,
             )
-            src = y[:].rearrange("m (v d) -> m d v", d=D)
-            dst = u[:, :, first // D : (first + width) // D]
+            src = y[:].rearrange("m (p q) -> m q p", q=TILES)
+            dst = u[:, h, :, col // TILES : (col + width) // TILES]
             if on_vector:
                 nc.vector.tensor_scalar(dst, src, -0.7, mkt_col[:], ALU.mult, ALU.add)
             else:
@@ -115,49 +116,60 @@ def tile_picked_ytranch_soft_p_kernel(tc, x_words, x_scales, w1, thr, mkt, lgd, 
                 product(words[:], CHUNK * c, CHUNK, f"bank{c}", c == CHUNKS - 2)
         nc.vector.tensor_tensor(ends[:, 1, :], ends[:, 0, :], wid_sb[:], ALU.add)
 
-        for bank, members in (("bank5", (0,)), ("bank0", (1,)), ("bank1", (2, 3)), ("bank2", (4, 5)), ("bank3", (6, 7))):
-            u_t = psum.tile([P, len(members), M], F32, name=f"u_t{members[0]}", tag=bank)
-            for e, d in enumerate(members):
-                nc.tensor.transpose(u_t[:, e, :], u[:, d, :], ident[:])
-            for e, d in enumerate(members):
-                nc.scalar.activation(th[:, d, :], u_t[:, e, :], ACT.Tanh, bias=thr_scaled[:, d : d + 1], scale=0.85)
+        banks = (("bank5", "bank0", "bank1"), ("bank2", "bank3", "bank4"))
+        for h in range(HALVES):
+            for bank, members in zip(banks[h], ((0,), (1,), (2, 3))):
+                u_t = psum.tile([P, len(members), M], F32, name=f"u_t{h}{members[0]}", tag=bank)
+                for e, q in enumerate(members):
+                    nc.tensor.transpose(u_t[:, e, :], u[:, h, q, :], ident[:])
+                for e, q in enumerate(members):
+                    nc.scalar.activation(th[:, h, q, :], u_t[:, e, :], ACT.Tanh, bias=thr_scaled[:, h, q : q + 1], scale=0.85)
 
-        nc.tensor.matmul(var_sum[:], peak_sum[:].to_broadcast([P, M]), ident[:], start=True, stop=False, is_transpose=True)
-        for d in range(D):
-            nc.vector.scalar_tensor_tensor(dip[:, d, :], th[:, d, :], neg_peak[:, d : d + 1], th[:, d, :], ALU.mult, ALU.mult)
-            nc.tensor.matmul(var_sum[:], dip[:, d, :], ident[:], start=False, stop=d == D - 1, is_transpose=True)
-        for d in range(D):
-            half = lgd_half[:, d : d + 1]
-            nc.vector.tensor_scalar(el[:, d, :], th[:, d, :], half, half, ALU.mult, ALU.add)
-            nc.tensor.matmul(loss[:], el[:, d, :], ident[:], start=d == 0, stop=d == D - 1, is_transpose=True)
+        for h in range(HALVES):
+            spread = peak_sum[:, h : h + 1].to_broadcast([P, M])
+            nc.tensor.matmul(var_sum[:, h, :], spread, ident[:], start=True, stop=False, is_transpose=True)
+            for q in range(TILES):
+                t = th[:, h, q, :]
+                nc.vector.scalar_tensor_tensor(dip[:, h, q, :], t, neg_peak[:, h, q : q + 1], t, ALU.mult, ALU.mult)
+                nc.tensor.matmul(var_sum[:, h, :], dip[:, h, q, :], ident[:], start=False, stop=q == TILES - 1, is_transpose=True)
+        var = keep.tile([P, V], F32, name="var")
+        nc.vector.tensor_reduce(var[:], var_sum[:].rearrange("m h (v e) -> m (h v) e", e=REST), AX.X, ALU.add)
+        for h in range(HALVES):
+            for q in range(TILES):
+                half = lgd_half[:, h, q : q + 1]
+                nc.vector.tensor_scalar(el[:, h, q, :], th[:, h, q, :], half, half, ALU.mult, ALU.add)
+                nc.tensor.matmul(el_sum[:, h, :], el[:, h, q, :], ident[:], start=q == 0, stop=q == TILES - 1, is_transpose=True)
+        loss = keep.tile([P, V], F32, name="loss")
+        nc.vector.tensor_reduce(loss[:], el_sum[:].rearrange("m h (v e) -> m (h v) e", e=REST), AX.X, ALU.add)
 
-        sdl = keep.tile([P, V], F32, name="sdl")
         inv_sdl = keep.tile([P, V], F32, name="inv_sdl")
         over = keep.tile([P, 2, V], F32, name="over")
         dist = keep.tile([P, 2, V], F32, name="dist")
-        z_abs = keep.tile([P, 2, V], F32, name="z_abs")
+        z_abs = keep.tile([P, 2, V], F32, name="z_abs", tag="z_abs")
         sig = keep.tile([P, 2, V], F32, name="sig")
         lg = keep.tile([P, V], F32, name="lg")
-        relu_b = keep.tile([P, V], F32, name="relu_b")
-        hard = keep.tile([P, V], F32, name="hard")
         inv_sig = keep.tile([P, V], F32, name="inv_sig")
         ratio = keep.tile([P, V], F32, name="ratio")
         soft = keep.tile([P, V], F32, name="soft")
         res = keep.tile([P, V], F32, name="res")
 
-        nc.scalar.activation(inv_sdl[:], var_sum[:], ACT.Abs_reciprocal_sqrt, bias=0.02)
-        nc.vector.tensor_tensor(over[:], loss[:].unsqueeze(1).to_broadcast([P, 2, V]), ends[:], ALU.subtract)
-        over_flat = over[:].rearrange("m s v -> m (s v)")
-        nc.vector.scalar_tensor_tensor(dist[:].rearrange("m s v -> m (s v)"), over_flat, -1.0, over_flat, ALU.mult, ALU.max)
-        nc.vector.tensor_tensor(z_abs[:], dist[:], inv_sdl[:].unsqueeze(1).to_broadcast([P, 2, V]), ALU.mult)
+        nc.scalar.activation(inv_sdl[:], var[:], ACT.Abs_reciprocal_sqrt, bias=0.02)
+        for e in range(2):
+            nc.vector.tensor_tensor(over[:, e, :], loss[:], ends[:, e, :], ALU.subtract)
+        for e in range(2):
+            nc.vector.scalar_tensor_tensor(dist[:, e, :], over[:, e, :], -1.0, over[:, e, :], ALU.mult, ALU.max)
+        for e in range(2):
+            nc.vector.tensor_tensor(z_abs[:, e, :], dist[:, e, :], inv_sdl[:], ALU.mult)
         nc.scalar.activation(sig[:, 0, :], z_abs[:, 0, :], ACT.Sigmoid)
         nc.scalar.activation(sig[:, 1, :], z_abs[:, 1, :], ACT.Sigmoid)
         nc.vector.reciprocal(inv_sig[:], sig[:, 0, :])
         nc.vector.tensor_tensor(ratio[:], sig[:, 1, :], inv_sig[:], ALU.mult)
         nc.scalar.activation(lg[:], ratio[:], ACT.Ln)
-        nc.vector.scalar_tensor_tensor(sdl[:], var_sum[:], 0.02, inv_sdl[:], ALU.add, ALU.mult)
-        nc.vector.tensor_scalar(relu_b[:], over[:, 1, :], 0.0, None, ALU.max)
-        nc.vector.scalar_tensor_tensor(hard[:], over[:, 0, :], 0.0, relu_b[:], ALU.max, ALU.subtract)
-        nc.vector.tensor_tensor(soft[:], lg[:], sdl[:], ALU.mult)
-        nc.vector.tensor_tensor(res[:], soft[:], hard[:], ALU.add)
+        late = keep.tile([P, 3, V], F32, name="late", tag="z_abs")
+        sdl, relu_b, hard = late[:, 0, :], late[:, 1, :], late[:, 2, :]
+        nc.vector.scalar_tensor_tensor(sdl, var[:], 0.02, inv_sdl[:], ALU.add, ALU.mult)
+        nc.vector.tensor_scalar(relu_b, over[:, 1, :], 0.0, None, ALU.max)
+        nc.vector.scalar_tensor_tensor(hard, over[:, 0, :], 0.0, relu_b, ALU.max, ALU.subtract)
+        nc.vector.tensor_tensor(soft[:], lg[:], sdl, ALU.mult)
+        nc.vector.tensor_tensor(res[:], soft[:], hard, ALU.add)
         nc.sync.dma_start(out, res[:])

@@ -43,9 +43,9 @@ def tile_picked_ytranch_soft_p_kernel(tc, x_words, x_scales, w1, thr, mkt, lgd, 
         ends = keep.tile([P, 2, V], F32, name="ends")
         wid_sb = keep.tile([P, V], F32, name="wid_sb")
 
-        nc.gpsimd.memset(table_scales[:].bitcast(I32), 0)
+        nc.gpsimd.memset(table_scales[:, : T // 2].bitcast(I32), 0)
+        nc.vector.memset(table_scales[:, T // 2 :].bitcast(I32), 0)
         nc.sync.dma_start(offsets[:], offs)
-        nc.sync.dma_start(ends[:, 0, :], att)
         for r in range(4):
             nc.sync.dma_start(table_scales[r:P:32, :].bitcast(I32), x_scales[0, r:16:4, :].bitcast(I32))
         nc.sync.dma_start(table_words[:].bitcast(I32), x_words[0].rearrange("p n t -> p (n t)").bitcast(I32))
@@ -53,6 +53,7 @@ def tile_picked_ytranch_soft_p_kernel(tc, x_words, x_scales, w1, thr, mkt, lgd, 
         nc.sync.dma_start(mkt_col[:], mkt)
         nc.sync.dma_start(thr_col[:], thr[0].rearrange("(h p q) -> p h q", h=HALVES, q=TILES))
         nc.sync.dma_start(lgd_col[:], lgd[0].rearrange("(h p q) -> p h q", h=HALVES, q=TILES))
+        nc.sync.dma_start(ends[:, 0, :], att)
         nc.sync.dma_start(wid_sb[:], wid)
 
         ident = keep.tile([P, P], F32, name="ident")
@@ -164,12 +165,16 @@ def tile_picked_ytranch_soft_p_kernel(tc, x_words, x_scales, w1, thr, mkt, lgd, 
         nc.scalar.activation(sig[:, 1, :], z_abs[:, 1, :], ACT.Sigmoid)
         nc.vector.reciprocal(inv_sig[:], sig[:, 0, :])
         nc.vector.tensor_tensor(ratio[:], sig[:, 1, :], inv_sig[:], ALU.mult)
-        nc.scalar.activation(lg[:], ratio[:], ACT.Ln)
+        sides = (slice(0, V // 2), slice(V // 2, V))
+        for side in sides:
+            nc.scalar.activation(lg[:, side], ratio[:, side], ACT.Ln)
         late = keep.tile([P, 3, V], F32, name="late", tag="z_abs")
         sdl, relu_b, hard = late[:, 0, :], late[:, 1, :], late[:, 2, :]
         nc.vector.scalar_tensor_tensor(sdl, var[:], 0.02, inv_sdl[:], ALU.add, ALU.mult)
         nc.vector.tensor_scalar(relu_b, over[:, 1, :], 0.0, None, ALU.max)
         nc.vector.scalar_tensor_tensor(hard, over[:, 0, :], 0.0, relu_b, ALU.max, ALU.subtract)
-        nc.vector.tensor_tensor(soft[:], lg[:], sdl, ALU.mult)
-        nc.vector.tensor_tensor(res[:], soft[:], hard, ALU.add)
+        for side in sides:
+            nc.vector.tensor_tensor(soft[:, side], lg[:, side], sdl[:, side], ALU.mult)
+        for side in sides:
+            nc.vector.tensor_tensor(res[:, side], soft[:, side], hard[:, side], ALU.add)
         nc.sync.dma_start(out, res[:])

from contextlib import ExitStack

import concourse.mybir as mybir
from concourse.masks import make_identity

K, T, S, D, M, V = 512, 2048, 1024, 8, 128, 128
FLOPS = 2 * K * M * S

F32 = mybir.dt.float32
BF16 = mybir.dt.bfloat16
I32 = mybir.dt.int32
U32 = mybir.dt.uint32
U16 = mybir.dt.uint16
U8 = mybir.dt.uint8
FP8X4 = mybir.dt.float8_e4m3fn_x4
ALU = mybir.AluOpType
ACT = mybir.ActivationFunctionType
AX = mybir.AxisListType

P = 128
PACK = 4
CHUNK = 256
CHUNKS = S // CHUNK
HALVES = 2
HALF = S // HALVES
TILES = HALF // P
REST = D // TILES


def tile_picked_ytranch_soft_p_kernel(tc, x_words, x_scales, w1, thr, mkt, lgd, att, wid, offs, out):
    nc = tc.nc
    with ExitStack() as ctx:
        keep = ctx.enter_context(tc.tile_pool(name="keep", bufs=1))
        psum = ctx.enter_context(tc.psum_pool(name="psum", bufs=1))

        offsets = keep.tile([P, S // 16], U16, name="offsets")
        table_scales = keep.tile([P, T], U8, name="table_scales", align_bytes=64)
        table_words = keep.tile([P, T], U32, name="table_words", align_bytes=64)
        w_raw = keep.tile([P, PACK, M], F32, name="w_raw")
        mkt_col = keep.tile([P, 1], F32, name="mkt_col")
        thr_col = keep.tile([P, HALVES, TILES], F32, name="thr_col")
        lgd_col = keep.tile([P, HALVES, TILES], F32, name="lgd_col")
        ends = keep.tile([P, 2, V], F32, name="ends")
        wid_sb = keep.tile([P, V], F32, name="wid_sb")

        nc.gpsimd.memset(table_scales[:, : T // 2].bitcast(I32), 0)
        nc.vector.memset(table_scales[:, T // 2 :].bitcast(I32), 0)
        nc.sync.dma_start(offsets[:], offs)
        for r in range(4):
            nc.sync.dma_start(table_scales[r:P:32, :].bitcast(I32), x_scales[0, r:16:4, :].bitcast(I32))
        nc.sync.dma_start(table_words[:].bitcast(I32), x_words[0].rearrange("p n t -> p (n t)").bitcast(I32))
        nc.sync.dma_start(w_raw[:], w1.rearrange("(p j) m -> p j m", j=PACK))
        nc.sync.dma_start(mkt_col[:], mkt)
        nc.sync.dma_start(thr_col[:], thr[0].rearrange("(h p q) -> p h q", h=HALVES, q=TILES))
        nc.sync.dma_start(lgd_col[:], lgd[0].rearrange("(h p q) -> p h q", h=HALVES, q=TILES))
        nc.sync.dma_start(ends[:, 0, :], att)
        nc.sync.dma_start(wid_sb[:], wid)

        ident = keep.tile([P, P], F32, name="ident")
        make_identity(nc, ident[:])

        w_bf = keep.tile([P, M, PACK], BF16, name="w_bf", tag="staged", align_bytes=64)
        w_codes = keep.tile([P, M], U32, name="w_codes", align_bytes=64)
        w_scales = keep.tile([P, M], U8, name="w_scales", align_bytes=64)
        nc.scalar.copy(w_bf[:], w_raw[:].rearrange("p j m -> p m j"))

        thr_scaled = keep.tile([P, HALVES, TILES], F32, name="thr_scaled")
        lgd_half = keep.tile([P, HALVES, TILES], F32, name="lgd_half")
        peak = keep.tile([P, HALVES, TILES], F32, name="peak")
        neg_peak = keep.tile([P, HALVES, TILES], F32, name="neg_peak")
        peak_sum = keep.tile([P, HALVES], F32, name="peak_sum")
        nc.scalar.mul(thr_scaled[:], thr_col[:], 0.85)
        for h in range(HALVES):
            nc.scalar.activation(peak[:, h, :], lgd_col[:, h, :], ACT.Square, scale=0.5, accum_out=peak_sum[:, h : h + 1])
        nc.scalar.mul(lgd_half[:], lgd_col[:], 0.5)
        nc.scalar.mul(neg_peak[:], peak[:], -1.0)

        picked_scales = [keep.tile([P, 2 * CHUNK], U8, name=f"picked_scales{h}", align_bytes=64) for h in range(2)]
        for h in range(2):
            nc.vector.tensor_copy(picked_scales[h][:], table_scales[:].indirect(offsets[:, 32 * h : 32 * h + 32]))
        nc.vector.quantize_mx(out=w_codes[:].bitcast(FP8X4), scales=w_scales[:], in_=w_bf[:].rearrange("p m j -> p (m j)"))

        u = keep.tile([P, HALVES, TILES, P], F32, name="u")
        th = keep.tile([P, HALVES, TILES, M], F32, name="th")
        el = keep.tile([P, HALVES, TILES, M], F32, name="el")
        dip = keep.tile([P, HALVES, TILES, M], F32, name="dip")
        var_sum = psum.tile([P, HALVES, P], F32, name="var_sum")
        el_sum = psum.tile([P, HALVES, P], F32, name="el_sum")

        def product(words, first, width, bank, on_vector):
            h, col = divmod(first, 2 * CHUNK)
            y = psum.tile([P, width], F32, name=f"y{first}", tag=bank)
            nc.tensor.matmul_mx(
                out=y[:],
                lhsT=w_codes[:].bitcast(FP8X4),
                lhsT_scale=w_scales[:],
                rhs=words.bitcast(FP8X4),
                rhs_scale=picked_scales[h][:, col : col + width],
                start=True,
                stop=True,
            )
            src = y[:].rearrange("m (p q) -> m q p", q=TILES)
            dst = u[:, h, :, col // TILES : (col + width) // TILES]
            if on_vector:
                nc.vector.tensor_scalar(dst, src, -0.7, mkt_col[:], ALU.mult, ALU.add)
            else:
                nc.scalar.activation(dst, src, ACT.Identity, bias=mkt_col[:], scale=-0.7)

        for c in range(CHUNKS):
            last = c == CHUNKS - 1
            words = keep.tile([P, CHUNK], U32, name=f"picked_words{c}", tag="staged" if last else f"words{c}", align_bytes=64)
            nc.vector.tensor_copy(words[:], table_words[:].indirect(offsets[:, 16 * c : 16 * c + 16]))
            if last:
                product(words[:, :P], CHUNK * c, P, "bank3", True)
                product(words[:, P:], CHUNK * c + P, P, "bank4", False)
            else:
                product(words[:], CHUNK * c, CHUNK, f"bank{c}", c == CHUNKS - 2)
        nc.vector.tensor_tensor(ends[:, 1, :], ends[:, 0, :], wid_sb[:], ALU.add)

        banks = (("bank5", "bank0", "bank1"), ("bank2", "bank3", "bank4"))
        for h in range(HALVES):
            for bank, members in zip(banks[h], ((0,), (1,), (2, 3))):
                u_t = psum.tile([P, len(members), M], F32, name=f"u_t{h}{members[0]}", tag=bank)
                for e, q in enumerate(members):
                    nc.tensor.transpose(u_t[:, e, :], u[:, h, q, :], ident[:])
                for e, q in enumerate(members):
                    nc.scalar.activation(th[:, h, q, :], u_t[:, e, :], ACT.Tanh, bias=thr_scaled[:, h, q : q + 1], scale=0.85)

        for h in range(HALVES):
            spread = peak_sum[:, h : h + 1].to_broadcast([P, M])
            nc.tensor.matmul(var_sum[:, h, :], spread, ident[:], start=True, stop=False, is_transpose=True)
            for q in range(TILES):
                t = th[:, h, q, :]
                nc.vector.scalar_tensor_tensor(dip[:, h, q, :], t, neg_peak[:, h, q : q + 1], t, ALU.mult, ALU.mult)
                nc.tensor.matmul(var_sum[:, h, :], dip[:, h, q, :], ident[:], start=False, stop=q == TILES - 1, is_transpose=True)
        var = keep.tile([P, V], F32, name="var")
        nc.vector.tensor_reduce(var[:], var_sum[:].rearrange("m h (v e) -> m (h v) e", e=REST), AX.X, ALU.add)
        for h in range(HALVES):
            for q in range(TILES):
                half = lgd_half[:, h, q : q + 1]
                nc.vector.tensor_scalar(el[:, h, q, :], th[:, h, q, :], half, half, ALU.mult, ALU.add)
                nc.tensor.matmul(el_sum[:, h, :], el[:, h, q, :], ident[:], start=q == 0, stop=q == TILES - 1, is_transpose=True)
        loss = keep.tile([P, V], F32, name="loss")
        nc.vector.tensor_reduce(loss[:], el_sum[:].rearrange("m h (v e) -> m (h v) e", e=REST), AX.X, ALU.add)

        inv_sdl = keep.tile([P, V], F32, name="inv_sdl")
        over = keep.tile([P, 2, V], F32, name="over")
        dist = keep.tile([P, 2, V], F32, name="dist")
        z_abs = keep.tile([P, 2, V], F32, name="z_abs", tag="z_abs")
        sig = keep.tile([P, 2, V], F32, name="sig")
        lg = keep.tile([P, V], F32, name="lg")
        inv_sig = keep.tile([P, V], F32, name="inv_sig")
        ratio = keep.tile([P, V], F32, name="ratio")
        soft = keep.tile([P, V], F32, name="soft")
        res = keep.tile([P, V], F32, name="res")

        nc.scalar.activation(inv_sdl[:], var[:], ACT.Abs_reciprocal_sqrt, bias=0.02)
        for e in range(2):
            nc.vector.tensor_tensor(over[:, e, :], loss[:], ends[:, e, :], ALU.subtract)
        for e in range(2):
            nc.vector.scalar_tensor_tensor(dist[:, e, :], over[:, e, :], -1.0, over[:, e, :], ALU.mult, ALU.max)
        for e in range(2):
            nc.vector.tensor_tensor(z_abs[:, e, :], dist[:, e, :], inv_sdl[:], ALU.mult)
        nc.scalar.activation(sig[:, 0, :], z_abs[:, 0, :], ACT.Sigmoid)
        nc.scalar.activation(sig[:, 1, :], z_abs[:, 1, :], ACT.Sigmoid)
        nc.vector.reciprocal(inv_sig[:], sig[:, 0, :])
        nc.vector.tensor_tensor(ratio[:], sig[:, 1, :], inv_sig[:], ALU.mult)
        sides = (slice(0, V // 2), slice(V // 2, V))
        for side in sides:
            nc.scalar.activation(lg[:, side], ratio[:, side], ACT.Ln)
        late = keep.tile([P, 3, V], F32, name="late", tag="z_abs")
        sdl, relu_b, hard = late[:, 0, :], late[:, 1, :], late[:, 2, :]
        nc.vector.scalar_tensor_tensor(sdl, var[:], 0.02, inv_sdl[:], ALU.add, ALU.mult)
        nc.vector.tensor_scalar(relu_b, over[:, 1, :], 0.0, None, ALU.max)
        nc.vector.scalar_tensor_tensor(hard, over[:, 0, :], 0.0, relu_b, ALU.max, ALU.subtract)
        for side in sides:
            nc.vector.tensor_tensor(soft[:, side], lg[:, side], sdl[:, side], ALU.mult)
        for side in sides:
            nc.vector.tensor_tensor(res[:, side], soft[:, side], hard[:, side], ALU.add)
        nc.sync.dma_start(out, res[:])
